import numpy as np
import ml_dtypes


def mxq(x, axis, fmt="e4m3"):
    dtype, down = {"e4m3": (ml_dtypes.float8_e4m3fn, 7), "e5m2": (ml_dtypes.float8_e5m2, 14)}[fmt]
    v = np.moveaxis(np.asarray(x, np.float32).astype(ml_dtypes.bfloat16).astype(np.float64), axis, -1)
    blocks = v.reshape(v.shape[:-1] + (-1, 32))
    amax = np.abs(blocks).max(-1, keepdims=True)
    byte = np.maximum(np.where(amax > 0, np.frexp(amax)[1] - 1 + 127, 0) - down, 1)
    scale = np.exp2(byte - 127.0)
    codes = (blocks / scale).astype(np.float32).astype(dtype).astype(np.float64)
    return np.moveaxis((codes * scale).reshape(v.shape), -1, axis)


WIDE = False


def mx_kscale(k):
    if not WIDE:
        return np.ones(k)
    levels = np.array([30, -30])
    if k % 512:
        return np.exp2(np.random.permutation(np.resize(levels, k // 32))).repeat(32)
    a = np.empty((k // 512, 16))
    for p in range(k // 512):
        a[p, :8] = np.random.permutation(np.resize(levels, 8))
        for g in range(8):
            far = levels[np.abs(levels - a[p, g]) >= 10]
            a[p, g + 8] = far[np.random.randint(len(far))]
    return np.exp2(a.ravel()).repeat(32)


def f64(x):
    return np.asarray(x).astype(np.float64)


def striped(idx):
    return np.tile(np.asarray(idx).reshape(-1, 16).T, (8, 1)).astype(np.uint16)


def unstriped(offs):
    return offs[:16].T.reshape(-1).astype(np.int64)


E2M1 = np.array([0.0, 0.5, 1.0, 1.5, 2.0, 3.0, 4.0, 6.0, -0.0, -0.5, -1.0, -1.5, -2.0, -3.0, -4.0, -6.0])


def pack_weight(w, fmt):
    k, n = w.shape
    w = f64(np.asarray(w, np.float32).astype(ml_dtypes.bfloat16)).reshape(k // 32, 32, n)
    amax = np.abs(w).max(1)
    if fmt in ("e4m3", "e5m2"):
        byte = np.frexp(amax)[1] - 1 + 127 - (7 if fmt == "e4m3" else 14)
    else:
        mant, ex = np.frexp(amax / 6.0)
        byte = np.where(mant > 0.5, ex, ex - 1) + 127
    byte = np.clip(np.where(amax > 0, byte, 1), 1, 254)
    scaled = (w * np.exp2(127.0 - byte)[:, None, :]).reshape(k, n).astype(np.float32)
    by_word = np.ascontiguousarray(scaled.reshape(k // 512, 128, 4, n).transpose(0, 1, 3, 2))
    if fmt in ("e4m3", "e5m2"):
        words = by_word.astype(ml_dtypes.float8_e4m3fn if fmt == "e4m3" else ml_dtypes.float8_e5m2).view(np.uint8)
    else:
        c = by_word.astype(ml_dtypes.float4_e2m1fn).view(np.uint8) & 0xF
        words = (c[..., 0::2] | (c[..., 1::2] << 4)).reshape(k // 512, 128, 2 * n)
    return np.ascontiguousarray(words), np.ascontiguousarray(byte.astype(np.uint8).reshape(k // 512, 16, n))


def unpack_weight(words, scales, fmt):
    g, _, n = scales.shape
    words = np.ascontiguousarray(words).reshape(g, 128, n, -1)
    if fmt in ("e4m3", "e5m2"):
        vals = words.view(ml_dtypes.float8_e4m3fn if fmt == "e4m3" else ml_dtypes.float8_e5m2).astype(np.float64)
    else:
        nib = np.empty((g, 128, n, 4), np.uint8)
        nib[..., 0::2] = words & 0xF
        nib[..., 1::2] = words >> 4
        vals = E2M1[nib]
    vals = vals * np.repeat(np.exp2(scales.astype(np.float64) - 127.0), 8, axis=1)[..., None]
    return vals.transpose(0, 1, 3, 2).reshape(g * 512, n)


def bf(x):
    return np.asarray(x, np.float32).astype(ml_dtypes.bfloat16)


def planes(Y):
    r, m = Y.shape
    b = f64(bf(Y)).reshape(r // 32, 32, m)
    amax = np.abs(b).max(1)
    byte = np.clip(np.where(amax > 0, np.frexp(amax)[1] - 1 + 127 - 7, 1), 1, 254)
    codes = (b * np.exp2(127.0 - byte)[:, None, :]).reshape(r, m).astype(np.float32).astype(ml_dtypes.float8_e4m3fn).view(np.uint8)
    words = codes.reshape(r // 512, 128, 4, m).transpose(0, 1, 3, 2)
    return np.ascontiguousarray(words), np.ascontiguousarray(byte.astype(np.uint8).reshape(r // 512, 16, m))


K, T, J, S, R, F, Z, N = 512, 512, 128, 512, 512, 512, 1024, 512


def setup_inputs():
    n = np.random.standard_normal
    idx = np.random.permutation(T)[:J]
    idx2 = np.random.permutation(S)[:J]
    idx3 = np.random.permutation(Z)[:J]
    fk = mx_kscale(K)
    fr = mx_kscale(R)
    ff = mx_kscale(F)
    wp = pack_weight(n((K, R)) * 1 / np.sqrt(K) * fk[:, None] * fr, "e5m2")
    xop = pack_weight(n((F, Z)) / ff[:, None], "e4m3")
    w2p = pack_weight(n((F, R)) * 1 / np.sqrt(F) * ff[:, None] * fr, "e5m2")
    wbp = pack_weight(n((R, N)) * 1 / np.sqrt(R) / fr[:, None], "e4m3")
    return {
        "xa": (n((K, T))).astype(np.float32),
        "xb": (n((K, S))).astype(np.float32),
        "hb": (np.random.uniform(0.2, 0.9, (K, 1))).astype(np.float32),
        "fk": (np.random.uniform(0.5, 2.0, (K, 1)) / fk[:, None]).astype(np.float32),
        "w_words": wp[0],
        "w_scales": wp[1],
        "xo_words": xop[0],
        "xo_scales": xop[1],
        "w2_words": w2p[0],
        "w2_scales": w2p[1],
        "wb_words": wbp[0],
        "wb_scales": wbp[1],
        "rs": (n((N, J))).astype(np.float32),
        "offs": striped(idx),
        "offs2": striped(idx2),
        "offs3": striped(idx3),
    }


def reference(xa, xb, hb, fk, w_words, w_scales, xo_words, xo_scales, w2_words, w2_scales, wb_words, wb_scales, rs, offs, offs2, offs3):
    idx = unstriped(offs)
    idx2 = unstriped(offs2)
    idx3 = unstriped(offs3)
    wu = unpack_weight(w_words, w_scales, "e5m2")
    xou = unpack_weight(xo_words, xo_scales, "e4m3")
    w2u = unpack_weight(w2_words, w2_scales, "e5m2")
    wbu = unpack_weight(wb_words, wb_scales, "e4m3")
    u = (f64(xa)[:, idx] - np.minimum(f64(xb)[:, idx2], f64(hb))) * f64(fk)
    uq = mxq(u, 0, "e5m2")
    xoidx3g = xou[:, idx3]
    a = wu.T @ uq + w2u.T @ xoidx3g
    hid = np.maximum(a, 0.0)
    hidq = mxq(hid, 0, "e5m2")
    p = wbu.T @ hidq
    p1 = np.pad(p, ((0, 0), (1, 0)))[:, :J]
    y = p - 0.7 * p1 + 0.5 * f64(rs)
    words, scales = planes(y)
    return y, words, scales

@@ -1,0 +1,197 @@
+from contextlib import ExitStack
+
+import concourse.mybir as mybir
+
+F32 = mybir.dt.float32
+BF16 = mybir.dt.bfloat16
+I32 = mybir.dt.int32
+U32 = mybir.dt.uint32
+U16 = mybir.dt.uint16
+U8 = mybir.dt.uint8
+E4M3 = mybir.dt.float8_e4m3fn_x4
+E5M2 = mybir.dt.float8_e5m2_x4
+ALU = mybir.AluOpType
+ACT = mybir.ActivationFunctionType
+
+P = 128
+PACK = 4
+J = 128
+WIDTH = 512
+Z = 1024
+FLOPS = 3 * 2 * 512 * 512 * J
+
+
+def tile_list_sum_boundedgaps_othertable_plain_lagged_pl_kernel(
+    tc, xa, xb, hb, fk, w_words, w_scales, xo_words, xo_scales, w2_words, w2_scales, wb_words, wb_scales, rs,
+    offs, offs2, offs3, out_0, out_1, out_2,
+):
+    nc = tc.nc
+    with ExitStack() as ctx:
+        pool = ctx.enter_context(tc.tile_pool(name="pool", bufs=1))
+        psum = ctx.enter_context(tc.psum_pool(name="psum", bufs=1))
+
+        def sb(name, shape, dtype, tag=None):
+            return pool.tile(shape, dtype, name=name, tag=tag or name, align_bytes=64)
+
+        list_a = pool.tile([P, J // 16], U16, name="list_a")
+        list_b = pool.tile([P, J // 16], U16, name="list_b")
+        list_o = pool.tile([P, J // 16], U16, name="list_o")
+        hb_sb = sb("hb_sb", [P, PACK], F32)
+        fk_sb = sb("fk_sb", [P, PACK], F32)
+        xa_sb = [sb("xa%d" % h, [P, 2, WIDTH], F32) for h in range(2)]
+        xb_sb = [sb("xb%d" % h, [P, 2, WIDTH], F32) for h in range(2)]
+        xo_w = sb("xo_w", [P, Z], U32)
+        xo_s = sb("xo_s", [P, Z], U8)
+        raw_w = {n: sb("raw_w_" + n, [P, WIDTH], U32) for n in ("w", "w2", "wb")}
+        raw_s = {n: sb("raw_s_" + n, [P, WIDTH], U8) for n in ("w", "w2", "wb")}
+        dealt_w = {n: sb("dealt_w_" + n, [P, PACK, P], U32) for n in ("w", "w2", "wb")}
+        dealt_s = {}
+        rs_sb = sb("rs_sb", [P, PACK, J], F32)
+
+        def load_words(tile, words):
+            nc.sync.dma_start(out=tile[:].bitcast(I32), in_=words[0].rearrange("p n t -> p (n t)").bitcast(I32))
+
+        def load_scale_rows(queue, tile, scales, quad):
+            queue.dma_start(
+                out=tile[32 * quad : 32 * quad + 4, :].bitcast(I32),
+                in_=scales[0, 4 * quad : 4 * quad + 4, :].bitcast(I32),
+            )
+
+        nc.vector.memset(xo_s[:].bitcast(I32), 0)
+        nc.vector.memset(raw_s["w2"][:].bitcast(I32), 0)
+        nc.gpsimd.memset(raw_s["w"][:].bitcast(I32), 0)
+        nc.gpsimd.memset(raw_s["wb"][:].bitcast(I32), 0)
+
+        xa_rows = xa.rearrange("(p i) t -> p i t", i=PACK)
+        xb_rows = xb.rearrange("(p i) t -> p i t", i=PACK)
+
+        nc.sync.dma_start(list_b[:], offs2)
+        nc.scalar.dma_start(out=hb_sb[:], in_=hb.rearrange("(p i) o -> p (i o)", i=PACK))
+        nc.sync.dma_start(out=xb_sb[0][:], in_=xb_rows[:, 0:2, :])
+        nc.scalar.dma_start(out=fk_sb[:], in_=fk.rearrange("(p i) o -> p (i o)", i=PACK))
+        nc.sync.dma_start(list_a[:], offs)
+        load_scale_rows(nc.scalar, xo_s, xo_scales, 0)
+        nc.sync.dma_start(out=xb_sb[1][:], in_=xb_rows[:, 2:4, :])
+        load_scale_rows(nc.scalar, xo_s, xo_scales, 1)
+        for quad in range(2, 4):
+            load_scale_rows(nc.gpsimd, raw_s["w"], w_scales, quad)
+        for quad in range(4):
+            load_scale_rows(nc.gpsimd, raw_s["wb"], wb_scales, quad)
+        nc.sync.dma_start(out=xa_sb[0][:], in_=xa_rows[:, 0:2, :])
+        load_scale_rows(nc.scalar, xo_s, xo_scales, 2)
+        nc.sync.dma_start(list_o[:], offs3)
+        load_scale_rows(nc.scalar, xo_s, xo_scales, 3)
+        nc.sync.dma_start(out=xa_sb[1][:], in_=xa_rows[:, 2:4, :])
+        load_scale_rows(nc.scalar, raw_s["w2"], w2_scales, 0)
+        load_words(xo_w, xo_words)
+        load_scale_rows(nc.scalar, raw_s["w2"], w2_scales, 1)
+        load_words(raw_w["w2"], w2_words)
+        load_scale_rows(nc.scalar, raw_s["w2"], w2_scales, 2)
+        load_words(raw_w["w"], w_words)
+        load_scale_rows(nc.scalar, raw_s["w2"], w2_scales, 3)
+        load_words(raw_w["wb"], wb_words)
+        load_scale_rows(nc.scalar, raw_s["w"], w_scales, 0)
+        nc.sync.dma_start(out=rs_sb[:], in_=rs.rearrange("(p t) j -> p t j", t=PACK))
+        load_scale_rows(nc.scalar, raw_s["w"], w_scales, 1)
+
+        def gather_plane(out, table, lst, i):
+            window = table[i // 2][:, i % 2, :].indirect(lst[:])
+            nc.vector.tensor_copy(out[:, i, :], window)
+
+        def deal_scales(n, tag):
+            dealt_s.setdefault(n, sb("dealt_s_" + n, [P, PACK, P], U8, tag))
+            nc.vector.tensor_copy(
+                out=dealt_s[n][:].rearrange("p t q -> p q t"), in_=raw_s[n][:].rearrange("p (q t) -> p q t", t=PACK)
+            )
+
+        def deal_words_vector(n):
+            nc.vector.tensor_copy(
+                out=dealt_w[n][:].bitcast(I32).rearrange("p t q -> p q t"),
+                in_=raw_w[n][:].bitcast(I32).rearrange("p (q t) -> p q t", t=PACK),
+            )
+
+        def deal_words_scalar(n):
+            nc.scalar.copy(
+                out=dealt_w[n][:].rearrange("p t q -> p q t"), in_=raw_w[n][:].rearrange("p (q t) -> p q t", t=PACK)
+            )
+
+        picked_b = sb("picked_b", [P, PACK, J], F32)
+        picked_a = sb("picked_a", [P, PACK, J], F32)
+        bounded = sb("bounded", [P, PACK, J], F32)
+        u32 = sb("u32", [P, PACK, J], F32)
+        for i in range(PACK):
+            gather_plane(picked_b, xb_sb, list_b, i)
+        for i in range(PACK):
+            nc.vector.tensor_scalar(
+                bounded[:, i, :], picked_b[:, i, :], hb_sb[:, i : i + 1], fk_sb[:, i : i + 1], ALU.min, ALU.mult
+            )
+        deal_scales("w2", "picked_b")
+        xo_gs = sb("xo_gs", [P, J], U8)
+        nc.vector.tensor_copy(xo_gs[:], xo_s[:].indirect(list_o[:]))
+        for i in range(PACK):
+            gather_plane(picked_a, xa_sb, list_a, i)
+        for i in range(PACK):
+            nc.vector.scalar_tensor_tensor(
+                u32[:, i, :], picked_a[:, i, :], fk_sb[:, i : i + 1], bounded[:, i, :], ALU.mult, ALU.subtract
+            )
+        u16 = sb("u16", [P, J, PACK], BF16)
+        nc.vector.tensor_copy(out=u16[:], in_=u32[:].rearrange("p i j -> p j i"))
+        deal_scales("w", "picked_a")
+        xo_gw = sb("xo_gw", [P, J], U32)
+        nc.vector.tensor_copy(xo_gw[:], xo_w[:].indirect(list_o[:]))
+        u_codes = sb("u_codes", [P, J], U32)
+        u_scales = sb("u_scales", [P, J], U8)
+        nc.vector.quantize_mx(out=u_codes[:].bitcast(E5M2), scales=u_scales[:], in_=u16[:].rearrange("p j i -> p (j i)"))
+        deal_words_scalar("w2")
+        deal_words_vector("w")
+        deal_scales("wb", "u16")
+        deal_words_scalar("wb")
+
+        acc = psum.tile([P, PACK, J], F32, name="acc")
+        for t in range(PACK):
+            nc.tensor.matmul_mx(
+                out=acc[:, t, :], lhsT=dealt_w["w2"][:, t, :].bitcast(E5M2), lhsT_scale=dealt_s["w2"][:, t, :],
+                rhs=xo_gw[:].bitcast(E4M3), rhs_scale=xo_gs[:], start=(t == 0), stop=False,
+            )
+        for t in range(PACK):
+            nc.tensor.matmul_mx(
+                out=acc[:, t, :], lhsT=dealt_w["w"][:, t, :].bitcast(E5M2), lhsT_scale=dealt_s["w"][:, t, :],
+                rhs=u_codes[:].bitcast(E5M2), rhs_scale=u_scales[:], start=False, stop=(t == PACK - 1),
+            )
+        hid16 = sb("hid16", [P, J, PACK], BF16)
+        nc.vector.tensor_scalar(hid16[:], acc[:].rearrange("p t j -> p j t"), 0.0, None, ALU.max)
+        hid_codes = sb("hid_codes", [P, J], U32)
+        hid_scales = sb("hid_scales", [P, J], U8)
+        nc.vector.quantize_mx(
+            out=hid_codes[:].bitcast(E5M2), scales=hid_scales[:], in_=hid16[:].rearrange("p j t -> p (j t)")
+        )
+
+        y = sb("y", [P, PACK, J], F32)
+        prod = [psum.tile([P, 2, J], F32, name="prod%d" % h) for h in range(2)]
+        for t in range(PACK):
+            nc.tensor.matmul_mx(
+                out=prod[t // 2][:, t % 2, :], lhsT=dealt_w["wb"][:, t, :].bitcast(E4M3),
+                lhsT_scale=dealt_s["wb"][:, t, :], rhs=hid_codes[:].bitcast(E5M2), rhs_scale=hid_scales[:],
+                start=True, stop=True,
+            )
+        for h in range(2):
+            nc.vector.scalar_tensor_tensor(
+                y[:, 2 * h : 2 * h + 2, :], rs_sb[:, 2 * h : 2 * h + 2, :], 0.5, prod[h][:], ALU.mult, ALU.add
+            )
+        out_rows = out_0.rearrange("(p t) j -> p t j", t=PACK)
+        for h in range(2):
+            later = y[:, 2 * h : 2 * h + 2, 1:J]
+            nc.vector.scalar_tensor_tensor(later, prod[h][:, :, 0 : J - 1], -0.7, later, ALU.mult, ALU.add)
+        nc.sync.dma_start(out=out_rows, in_=y[:])
+        y16 = sb("y16", [P, J, PACK], BF16)
+        nc.vector.tensor_copy(out=y16[:], in_=y[:].rearrange("p t j -> p j t"))
+        y_codes = sb("y_codes", [P, J], U32)
+        y_scales = sb("y_scales", [P, J], U8)
+        nc.vector.quantize_mx(out=y_codes[:].bitcast(E4M3), scales=y_scales[:], in_=y16[:].rearrange("p j t -> p (j t)"))
+        nc.sync.dma_start(out=out_1[0].rearrange("p j t -> p (j t)").bitcast(I32), in_=y_codes[:].bitcast(I32))
+        for quad in range(4):
+            queue = nc.scalar if quad % 2 == 0 else nc.sync
+            queue.dma_start(
+                out=out_2[0, 4 * quad : 4 * quad + 4, :].bitcast(I32),
+                in_=y_scales[32 * quad : 32 * quad + 4, :].bitcast(I32),
+            )

@@ -16,8 +16,12 @@ ACT = mybir.ActivationFunctionType
 P = 128
 PACK = 4
 J = 128
+LIST_GROUP = 16
 WIDTH = 512
 Z = 1024
+QUADRANT = 32
+SCALE_ROWS = 4
+WEIGHTS = ("w", "w2", "wb")
 FLOPS = 3 * 2 * 512 * 512 * J
 
 
@@ -30,138 +34,139 @@ def tile_list_sum_boundedgaps_othertable_plain_lagged_pl_kernel(
         pool = ctx.enter_context(tc.tile_pool(name="pool", bufs=1))
         psum = ctx.enter_context(tc.psum_pool(name="psum", bufs=1))
 
-        def sb(name, shape, dtype, tag=None):
-            return pool.tile(shape, dtype, name=name, tag=tag or name, align_bytes=64)
+        def sb(name, shape, dtype, reuses=None):
+            return pool.tile(shape, dtype, name=name, tag=reuses or name, align_bytes=64)
 
-        list_a = pool.tile([P, J // 16], U16, name="list_a")
-        list_b = pool.tile([P, J // 16], U16, name="list_b")
-        list_o = pool.tile([P, J // 16], U16, name="list_o")
+        list_a = pool.tile([P, J // LIST_GROUP], U16, name="list_a")
+        list_b = pool.tile([P, J // LIST_GROUP], U16, name="list_b")
+        list_o = pool.tile([P, J // LIST_GROUP], U16, name="list_o")
         hb_sb = sb("hb_sb", [P, PACK], F32)
         fk_sb = sb("fk_sb", [P, PACK], F32)
         xa_sb = [sb("xa%d" % h, [P, 2, WIDTH], F32) for h in range(2)]
         xb_sb = [sb("xb%d" % h, [P, 2, WIDTH], F32) for h in range(2)]
         xo_w = sb("xo_w", [P, Z], U32)
         xo_s = sb("xo_s", [P, Z], U8)
-        raw_w = {n: sb("raw_w_" + n, [P, WIDTH], U32) for n in ("w", "w2", "wb")}
-        raw_s = {n: sb("raw_s_" + n, [P, WIDTH], U8) for n in ("w", "w2", "wb")}
-        dealt_w = {n: sb("dealt_w_" + n, [P, PACK, P], U32) for n in ("w", "w2", "wb")}
-        dealt_s = {}
+        raw_w = {n: sb("raw_w_" + n, [P, WIDTH], U32) for n in WEIGHTS}
+        raw_s = {n: sb("raw_s_" + n, [P, WIDTH], U8) for n in WEIGHTS}
+        dealt_w = {n: sb("dealt_w_" + n, [P, PACK, P], U32) for n in WEIGHTS}
         rs_sb = sb("rs_sb", [P, PACK, J], F32)
 
         def load_words(tile, words):
             nc.sync.dma_start(out=tile[:].bitcast(I32), in_=words[0].rearrange("p n t -> p (n t)").bitcast(I32))
 
-        def load_scale_rows(queue, tile, scales, quad):
-            queue.dma_start(
-                out=tile[32 * quad : 32 * quad + 4, :].bitcast(I32),
-                in_=scales[0, 4 * quad : 4 * quad + 4, :].bitcast(I32),
-            )
+        def load_scale_rows(tile, scales, quads):
+            for quad in quads:
+                nc.sync.dma_start(
+                    out=tile[QUADRANT * quad : QUADRANT * quad + SCALE_ROWS, :].bitcast(I32),
+                    in_=scales[0, SCALE_ROWS * quad : SCALE_ROWS * (quad + 1), :].bitcast(I32),
+                )
 
-        nc.vector.memset(xo_s[:].bitcast(I32), 0)
-        nc.vector.memset(raw_s["w2"][:].bitcast(I32), 0)
+        nc.gpsimd.memset(raw_s["w2"][:].bitcast(I32), 0)
         nc.gpsimd.memset(raw_s["w"][:].bitcast(I32), 0)
         nc.gpsimd.memset(raw_s["wb"][:].bitcast(I32), 0)
+        nc.vector.memset(xo_s[:].bitcast(I32), 0)
 
-        xa_rows = xa.rearrange("(p i) t -> p i t", i=PACK)
-        xb_rows = xb.rearrange("(p i) t -> p i t", i=PACK)
+        xa_planes = xa.rearrange("(p i) t -> p i t", i=PACK)
+        xb_planes = xb.rearrange("(p i) t -> p i t", i=PACK)
 
         nc.sync.dma_start(list_b[:], offs2)
-        nc.scalar.dma_start(out=hb_sb[:], in_=hb.rearrange("(p i) o -> p (i o)", i=PACK))
-        nc.sync.dma_start(out=xb_sb[0][:], in_=xb_rows[:, 0:2, :])
-        nc.scalar.dma_start(out=fk_sb[:], in_=fk.rearrange("(p i) o -> p (i o)", i=PACK))
+        nc.sync.dma_start(out=hb_sb[:], in_=hb.rearrange("(p i) o -> p (i o)", i=PACK))
+        nc.sync.dma_start(out=fk_sb[:], in_=fk.rearrange("(p i) o -> p (i o)", i=PACK))
+        nc.sync.dma_start(out=xb_sb[0][:], in_=xb_planes[:, 0:2, :])
         nc.sync.dma_start(list_a[:], offs)
-        load_scale_rows(nc.scalar, xo_s, xo_scales, 0)
-        nc.sync.dma_start(out=xb_sb[1][:], in_=xb_rows[:, 2:4, :])
-        load_scale_rows(nc.scalar, xo_s, xo_scales, 1)
-        for quad in range(2, 4):
-            load_scale_rows(nc.gpsimd, raw_s["w"], w_scales, quad)
-        for quad in range(4):
-            load_scale_rows(nc.gpsimd, raw_s["wb"], wb_scales, quad)
-        nc.sync.dma_start(out=xa_sb[0][:], in_=xa_rows[:, 0:2, :])
-        load_scale_rows(nc.scalar, xo_s, xo_scales, 2)
         nc.sync.dma_start(list_o[:], offs3)
-        load_scale_rows(nc.scalar, xo_s, xo_scales, 3)
-        nc.sync.dma_start(out=xa_sb[1][:], in_=xa_rows[:, 2:4, :])
-        load_scale_rows(nc.scalar, raw_s["w2"], w2_scales, 0)
+        load_scale_rows(raw_s["w2"], w2_scales, (0,))
+        nc.sync.dma_start(out=xb_sb[1][:], in_=xb_planes[:, 2:4, :])
+        load_scale_rows(raw_s["w2"], w2_scales, (1, 2))
+        nc.sync.dma_start(out=xa_sb[0][:], in_=xa_planes[:, 0:2, :])
+        load_scale_rows(raw_s["w2"], w2_scales, (3,))
+        load_scale_rows(xo_s, xo_scales, (0, 1))
+        nc.sync.dma_start(out=xa_sb[1][:], in_=xa_planes[:, 2:4, :])
+        load_scale_rows(xo_s, xo_scales, (2, 3))
         load_words(xo_w, xo_words)
-        load_scale_rows(nc.scalar, raw_s["w2"], w2_scales, 1)
+        load_scale_rows(raw_s["w"], w_scales, (0, 1))
         load_words(raw_w["w2"], w2_words)
-        load_scale_rows(nc.scalar, raw_s["w2"], w2_scales, 2)
+        load_scale_rows(raw_s["w"], w_scales, (2, 3))
         load_words(raw_w["w"], w_words)
-        load_scale_rows(nc.scalar, raw_s["w2"], w2_scales, 3)
+        load_scale_rows(raw_s["wb"], wb_scales, (0, 1))
         load_words(raw_w["wb"], wb_words)
-        load_scale_rows(nc.scalar, raw_s["w"], w_scales, 0)
+        load_scale_rows(raw_s["wb"], wb_scales, (2, 3))
         nc.sync.dma_start(out=rs_sb[:], in_=rs.rearrange("(p t) j -> p t j", t=PACK))
-        load_scale_rows(nc.scalar, raw_s["w"], w_scales, 1)
 
-        def gather_plane(out, table, lst, i):
-            window = table[i // 2][:, i % 2, :].indirect(lst[:])
-            nc.vector.tensor_copy(out[:, i, :], window)
+        def gather_plane(on_scalar, out, table, entries, i):
+            window = table[i // 2][:, i % 2, :].indirect(entries[:])
+            if on_scalar:
+                nc.scalar.activation(out[:, i, :], window, ACT.Copy)
+            else:
+                nc.vector.tensor_copy(out[:, i, :], window)
 
-        def deal_scales(n, tag):
-            dealt_s.setdefault(n, sb("dealt_s_" + n, [P, PACK, P], U8, tag))
+        def deal_scales(n, reuses):
+            dealt = sb("dealt_s_" + n, [P, PACK, P], U8, reuses)
             nc.vector.tensor_copy(
-                out=dealt_s[n][:].rearrange("p t q -> p q t"), in_=raw_s[n][:].rearrange("p (q t) -> p q t", t=PACK)
+                out=dealt[:].rearrange("p t q -> p q t"), in_=raw_s[n][:].rearrange("p (q t) -> p q t", t=PACK)
+            )
+            return dealt
+
+        def deal_words_on_vector(n, q_range):
+            nc.vector.tensor_copy(
+                out=dealt_w[n][:].bitcast(I32).rearrange("p t q -> p q t")[:, q_range, :],
+                in_=raw_w[n][:].bitcast(I32).rearrange("p (q t) -> p q t", t=PACK)[:, q_range, :],
             )
 
-        def deal_words_vector(n):
-            nc.vector.tensor_copy(
-                out=dealt_w[n][:].bitcast(I32).rearrange("p t q -> p q t"),
-                in_=raw_w[n][:].bitcast(I32).rearrange("p (q t) -> p q t", t=PACK),
-            )
-
-        def deal_words_scalar(n):
+        def deal_words_on_scalar(n, q_range):
             nc.scalar.copy(
-                out=dealt_w[n][:].rearrange("p t q -> p q t"), in_=raw_w[n][:].rearrange("p (q t) -> p q t", t=PACK)
+                out=dealt_w[n][:].rearrange("p t q -> p q t")[:, q_range, :],
+                in_=raw_w[n][:].rearrange("p (q t) -> p q t", t=PACK)[:, q_range, :],
             )
 
         picked_b = sb("picked_b", [P, PACK, J], F32)
         picked_a = sb("picked_a", [P, PACK, J], F32)
-        bounded = sb("bounded", [P, PACK, J], F32)
         u32 = sb("u32", [P, PACK, J], F32)
         for i in range(PACK):
-            gather_plane(picked_b, xb_sb, list_b, i)
+            gather_plane(i == 1, picked_b, xb_sb, list_b, i)
+        bounded = sb("bounded", [P, PACK, J], F32, reuses="xb1")
         for i in range(PACK):
             nc.vector.tensor_scalar(
                 bounded[:, i, :], picked_b[:, i, :], hb_sb[:, i : i + 1], fk_sb[:, i : i + 1], ALU.min, ALU.mult
             )
-        deal_scales("w2", "picked_b")
-        xo_gs = sb("xo_gs", [P, J], U8)
-        nc.vector.tensor_copy(xo_gs[:], xo_s[:].indirect(list_o[:]))
         for i in range(PACK):
-            gather_plane(picked_a, xa_sb, list_a, i)
+            gather_plane(i % 2 == 1, picked_a, xa_sb, list_a, i)
+        w2_dealt_s = deal_scales("w2", reuses="picked_b")
+        xo_picked_s = sb("xo_picked_s", [P, J], U8)
+        nc.vector.tensor_copy(xo_picked_s[:], xo_s[:].indirect(list_o[:]))
         for i in range(PACK):
             nc.vector.scalar_tensor_tensor(
                 u32[:, i, :], picked_a[:, i, :], fk_sb[:, i : i + 1], bounded[:, i, :], ALU.mult, ALU.subtract
             )
         u16 = sb("u16", [P, J, PACK], BF16)
         nc.vector.tensor_copy(out=u16[:], in_=u32[:].rearrange("p i j -> p j i"))
-        deal_scales("w", "picked_a")
-        xo_gw = sb("xo_gw", [P, J], U32)
-        nc.vector.tensor_copy(xo_gw[:], xo_w[:].indirect(list_o[:]))
+        xo_picked_w = sb("xo_picked_w", [P, J], U32)
+        nc.vector.tensor_copy(xo_picked_w[:], xo_w[:].indirect(list_o[:]))
         u_codes = sb("u_codes", [P, J], U32)
         u_scales = sb("u_scales", [P, J], U8)
         nc.vector.quantize_mx(out=u_codes[:].bitcast(E5M2), scales=u_scales[:], in_=u16[:].rearrange("p j i -> p (j i)"))
-        deal_words_scalar("w2")
-        deal_words_vector("w")
-        deal_scales("wb", "u16")
-        deal_words_scalar("wb")
+        w_dealt_s = deal_scales("w", reuses="u16")
+        deal_words_on_scalar("w2", slice(0, P))
+        deal_words_on_scalar("w", slice(0, P // 2))
+        deal_words_on_vector("w", slice(P // 2, P))
+        deal_words_on_vector("wb", slice(0, P))
+        wb_dealt_s = deal_scales("wb", reuses="raw_s_w")
 
         acc = psum.tile([P, PACK, J], F32, name="acc")
         for t in range(PACK):
             nc.tensor.matmul_mx(
-                out=acc[:, t, :], lhsT=dealt_w["w2"][:, t, :].bitcast(E5M2), lhsT_scale=dealt_s["w2"][:, t, :],
-                rhs=xo_gw[:].bitcast(E4M3), rhs_scale=xo_gs[:], start=(t == 0), stop=False,
+                out=acc[:, t, :], lhsT=dealt_w["w2"][:, t, :].bitcast(E5M2), lhsT_scale=w2_dealt_s[:, t, :],
+                rhs=xo_picked_w[:].bitcast(E4M3), rhs_scale=xo_picked_s[:], start=(t == 0), stop=False,
             )
         for t in range(PACK):
             nc.tensor.matmul_mx(
-                out=acc[:, t, :], lhsT=dealt_w["w"][:, t, :].bitcast(E5M2), lhsT_scale=dealt_s["w"][:, t, :],
+                out=acc[:, t, :], lhsT=dealt_w["w"][:, t, :].bitcast(E5M2), lhsT_scale=w_dealt_s[:, t, :],
                 rhs=u_codes[:].bitcast(E5M2), rhs_scale=u_scales[:], start=False, stop=(t == PACK - 1),
             )
         hid16 = sb("hid16", [P, J, PACK], BF16)
-        nc.vector.tensor_scalar(hid16[:], acc[:].rearrange("p t j -> p j t"), 0.0, None, ALU.max)
-        hid_codes = sb("hid_codes", [P, J], U32)
-        hid_scales = sb("hid_scales", [P, J], U8)
+        nc.scalar.activation(hid16[:], acc[:].rearrange("p t j -> p j t"), ACT.Relu)
+        hid_codes = sb("hid_codes", [P, J], U32, reuses="raw_w_wb")
+        hid_scales = sb("hid_scales", [P, J], U8, reuses="raw_s_wb")
         nc.vector.quantize_mx(
             out=hid_codes[:].bitcast(E5M2), scales=hid_scales[:], in_=hid16[:].rearrange("p j t -> p (j t)")
         )
@@ -171,27 +176,27 @@ def tile_list_sum_boundedgaps_othertable_plain_lagged_pl_kernel(
         for t in range(PACK):
             nc.tensor.matmul_mx(
                 out=prod[t // 2][:, t % 2, :], lhsT=dealt_w["wb"][:, t, :].bitcast(E4M3),
-                lhsT_scale=dealt_s["wb"][:, t, :], rhs=hid_codes[:].bitcast(E5M2), rhs_scale=hid_scales[:],
+                lhsT_scale=wb_dealt_s[:, t, :], rhs=hid_codes[:].bitcast(E5M2), rhs_scale=hid_scales[:],
                 start=True, stop=True,
             )
         for h in range(2):
             nc.vector.scalar_tensor_tensor(
                 y[:, 2 * h : 2 * h + 2, :], rs_sb[:, 2 * h : 2 * h + 2, :], 0.5, prod[h][:], ALU.mult, ALU.add
             )
-        out_rows = out_0.rearrange("(p t) j -> p t j", t=PACK)
         for h in range(2):
             later = y[:, 2 * h : 2 * h + 2, 1:J]
             nc.vector.scalar_tensor_tensor(later, prod[h][:, :, 0 : J - 1], -0.7, later, ALU.mult, ALU.add)
-        nc.sync.dma_start(out=out_rows, in_=y[:])
+        nc.sync.dma_start(out=out_0.rearrange("(p t) j -> p t j", t=PACK), in_=y[:])
+
         y16 = sb("y16", [P, J, PACK], BF16)
         nc.vector.tensor_copy(out=y16[:], in_=y[:].rearrange("p t j -> p j t"))
         y_codes = sb("y_codes", [P, J], U32)
         y_scales = sb("y_scales", [P, J], U8)
         nc.vector.quantize_mx(out=y_codes[:].bitcast(E4M3), scales=y_scales[:], in_=y16[:].rearrange("p j t -> p (j t)"))
         nc.sync.dma_start(out=out_1[0].rearrange("p j t -> p (j t)").bitcast(I32), in_=y_codes[:].bitcast(I32))
-        for quad in range(4):
+        for quad in range(P // QUADRANT):
             queue = nc.scalar if quad % 2 == 0 else nc.sync
             queue.dma_start(
-                out=out_2[0, 4 * quad : 4 * quad + 4, :].bitcast(I32),
-                in_=y_scales[32 * quad : 32 * quad + 4, :].bitcast(I32),
+                out=out_2[0, SCALE_ROWS * quad : SCALE_ROWS * (quad + 1), :].bitcast(I32),
+                in_=y_scales[QUADRANT * quad : QUADRANT * quad + SCALE_ROWS, :].bitcast(I32),
             )

from contextlib import ExitStack

import concourse.mybir as mybir

F32 = mybir.dt.float32
BF16 = mybir.dt.bfloat16
I32 = mybir.dt.int32
U32 = mybir.dt.uint32
U16 = mybir.dt.uint16
U8 = mybir.dt.uint8
E4M3 = mybir.dt.float8_e4m3fn_x4
E5M2 = mybir.dt.float8_e5m2_x4
ALU = mybir.AluOpType
ACT = mybir.ActivationFunctionType

P = 128
PACK = 4
J = 128
LIST_GROUP = 16
WIDTH = 512
Z = 1024
QUADRANT = 32
SCALE_ROWS = 4
WEIGHTS = ("w", "w2", "wb")
FLOPS = 3 * 2 * 512 * 512 * J


def tile_list_sum_boundedgaps_othertable_plain_lagged_pl_kernel(
    tc, xa, xb, hb, fk, w_words, w_scales, xo_words, xo_scales, w2_words, w2_scales, wb_words, wb_scales, rs,
    offs, offs2, offs3, out_0, out_1, out_2,
):
    nc = tc.nc
    with ExitStack() as ctx:
        pool = ctx.enter_context(tc.tile_pool(name="pool", bufs=1))
        psum = ctx.enter_context(tc.psum_pool(name="psum", bufs=1))

        def sb(name, shape, dtype, reuses=None):
            return pool.tile(shape, dtype, name=name, tag=reuses or name, align_bytes=64)

        list_a = pool.tile([P, J // LIST_GROUP], U16, name="list_a")
        list_b = pool.tile([P, J // LIST_GROUP], U16, name="list_b")
        list_o = pool.tile([P, J // LIST_GROUP], U16, name="list_o")
        hb_sb = sb("hb_sb", [P, PACK], F32)
        fk_sb = sb("fk_sb", [P, PACK], F32)
        xa_sb = [sb("xa%d" % h, [P, 2, WIDTH], F32) for h in range(2)]
        xb_sb = [sb("xb%d" % h, [P, 2, WIDTH], F32) for h in range(2)]
        xo_w = sb("xo_w", [P, Z], U32)
        xo_s = sb("xo_s", [P, Z], U8)
        raw_w = {n: sb("raw_w_" + n, [P, WIDTH], U32) for n in WEIGHTS}
        raw_s = {n: sb("raw_s_" + n, [P, WIDTH], U8) for n in WEIGHTS}
        dealt_w = {n: sb("dealt_w_" + n, [P, PACK, P], U32) for n in WEIGHTS}
        rs_sb = sb("rs_sb", [P, PACK, J], F32)

        def load_words(tile, words):
            nc.sync.dma_start(out=tile[:].bitcast(I32), in_=words[0].rearrange("p n t -> p (n t)").bitcast(I32))

        def load_scale_rows(tile, scales, quads):
            for quad in quads:
                nc.sync.dma_start(
                    out=tile[QUADRANT * quad : QUADRANT * quad + SCALE_ROWS, :].bitcast(I32),
                    in_=scales[0, SCALE_ROWS * quad : SCALE_ROWS * (quad + 1), :].bitcast(I32),
                )

        nc.gpsimd.memset(raw_s["w2"][:].bitcast(I32), 0)
        nc.gpsimd.memset(raw_s["w"][:].bitcast(I32), 0)
        nc.gpsimd.memset(raw_s["wb"][:].bitcast(I32), 0)
        nc.vector.memset(xo_s[:].bitcast(I32), 0)

        xa_planes = xa.rearrange("(p i) t -> p i t", i=PACK)
        xb_planes = xb.rearrange("(p i) t -> p i t", i=PACK)

        nc.sync.dma_start(list_b[:], offs2)
        nc.sync.dma_start(out=hb_sb[:], in_=hb.rearrange("(p i) o -> p (i o)", i=PACK))
        nc.sync.dma_start(out=fk_sb[:], in_=fk.rearrange("(p i) o -> p (i o)", i=PACK))
        nc.sync.dma_start(out=xb_sb[0][:], in_=xb_planes[:, 0:2, :])
        nc.sync.dma_start(list_a[:], offs)
        nc.sync.dma_start(list_o[:], offs3)
        load_scale_rows(raw_s["w2"], w2_scales, (0,))
        nc.sync.dma_start(out=xb_sb[1][:], in_=xb_planes[:, 2:4, :])
        load_scale_rows(raw_s["w2"], w2_scales, (1, 2))
        nc.sync.dma_start(out=xa_sb[0][:], in_=xa_planes[:, 0:2, :])
        load_scale_rows(raw_s["w2"], w2_scales, (3,))
        load_scale_rows(xo_s, xo_scales, (0, 1))
        nc.sync.dma_start(out=xa_sb[1][:], in_=xa_planes[:, 2:4, :])
        load_scale_rows(xo_s, xo_scales, (2, 3))
        load_words(xo_w, xo_words)
        load_scale_rows(raw_s["w"], w_scales, (0, 1))
        load_words(raw_w["w2"], w2_words)
        load_scale_rows(raw_s["w"], w_scales, (2, 3))
        load_words(raw_w["w"], w_words)
        load_scale_rows(raw_s["wb"], wb_scales, (0, 1))
        load_words(raw_w["wb"], wb_words)
        load_scale_rows(raw_s["wb"], wb_scales, (2, 3))
        nc.sync.dma_start(out=rs_sb[:], in_=rs.rearrange("(p t) j -> p t j", t=PACK))

        def gather_plane(on_scalar, out, table, entries, i):
            window = table[i // 2][:, i % 2, :].indirect(entries[:])
            if on_scalar:
                nc.scalar.activation(out[:, i, :], window, ACT.Copy)
            else:
                nc.vector.tensor_copy(out[:, i, :], window)

        def deal_scales(n, reuses):
            dealt = sb("dealt_s_" + n, [P, PACK, P], U8, reuses)
            nc.vector.tensor_copy(
                out=dealt[:].rearrange("p t q -> p q t"), in_=raw_s[n][:].rearrange("p (q t) -> p q t", t=PACK)
            )
            return dealt

        def deal_words_on_vector(n, q_range):
            nc.vector.tensor_copy(
                out=dealt_w[n][:].bitcast(I32).rearrange("p t q -> p q t")[:, q_range, :],
                in_=raw_w[n][:].bitcast(I32).rearrange("p (q t) -> p q t", t=PACK)[:, q_range, :],
            )

        def deal_words_on_scalar(n, q_range):
            nc.scalar.copy(
                out=dealt_w[n][:].rearrange("p t q -> p q t")[:, q_range, :],
                in_=raw_w[n][:].rearrange("p (q t) -> p q t", t=PACK)[:, q_range, :],
            )

        picked_b = sb("picked_b", [P, PACK, J], F32)
        picked_a = sb("picked_a", [P, PACK, J], F32)
        u32 = sb("u32", [P, PACK, J], F32)
        for i in range(PACK):
            gather_plane(i == 1, picked_b, xb_sb, list_b, i)
        bounded = sb("bounded", [P, PACK, J], F32, reuses="xb1")
        for i in range(PACK):
            nc.vector.tensor_scalar(
                bounded[:, i, :], picked_b[:, i, :], hb_sb[:, i : i + 1], fk_sb[:, i : i + 1], ALU.min, ALU.mult
            )
        for i in range(PACK):
            gather_plane(i % 2 == 1, picked_a, xa_sb, list_a, i)
        w2_dealt_s = deal_scales("w2", reuses="picked_b")
        xo_picked_s = sb("xo_picked_s", [P, J], U8)
        nc.vector.tensor_copy(xo_picked_s[:], xo_s[:].indirect(list_o[:]))
        for i in range(PACK):
            nc.vector.scalar_tensor_tensor(
                u32[:, i, :], picked_a[:, i, :], fk_sb[:, i : i + 1], bounded[:, i, :], ALU.mult, ALU.subtract
            )
        u16 = sb("u16", [P, J, PACK], BF16)
        nc.vector.tensor_copy(out=u16[:], in_=u32[:].rearrange("p i j -> p j i"))
        xo_picked_w = sb("xo_picked_w", [P, J], U32)
        nc.vector.tensor_copy(xo_picked_w[:], xo_w[:].indirect(list_o[:]))
        u_codes = sb("u_codes", [P, J], U32)
        u_scales = sb("u_scales", [P, J], U8)
        nc.vector.quantize_mx(out=u_codes[:].bitcast(E5M2), scales=u_scales[:], in_=u16[:].rearrange("p j i -> p (j i)"))
        w_dealt_s = deal_scales("w", reuses="u16")
        deal_words_on_scalar("w2", slice(0, P))
        deal_words_on_scalar("w", slice(0, P // 2))
        deal_words_on_vector("w", slice(P // 2, P))
        deal_words_on_vector("wb", slice(0, P))
        wb_dealt_s = deal_scales("wb", reuses="raw_s_w")

        acc = psum.tile([P, PACK, J], F32, name="acc")
        for t in range(PACK):
            nc.tensor.matmul_mx(
                out=acc[:, t, :], lhsT=dealt_w["w2"][:, t, :].bitcast(E5M2), lhsT_scale=w2_dealt_s[:, t, :],
                rhs=xo_picked_w[:].bitcast(E4M3), rhs_scale=xo_picked_s[:], start=(t == 0), stop=False,
            )
        for t in range(PACK):
            nc.tensor.matmul_mx(
                out=acc[:, t, :], lhsT=dealt_w["w"][:, t, :].bitcast(E5M2), lhsT_scale=w_dealt_s[:, t, :],
                rhs=u_codes[:].bitcast(E5M2), rhs_scale=u_scales[:], start=False, stop=(t == PACK - 1),
            )
        hid16 = sb("hid16", [P, J, PACK], BF16)
        nc.scalar.activation(hid16[:], acc[:].rearrange("p t j -> p j t"), ACT.Relu)
        hid_codes = sb("hid_codes", [P, J], U32, reuses="raw_w_wb")
        hid_scales = sb("hid_scales", [P, J], U8, reuses="raw_s_wb")
        nc.vector.quantize_mx(
            out=hid_codes[:].bitcast(E5M2), scales=hid_scales[:], in_=hid16[:].rearrange("p j t -> p (j t)")
        )

        y = sb("y", [P, PACK, J], F32)
        prod = [psum.tile([P, 2, J], F32, name="prod%d" % h) for h in range(2)]
        for t in range(PACK):
            nc.tensor.matmul_mx(
                out=prod[t // 2][:, t % 2, :], lhsT=dealt_w["wb"][:, t, :].bitcast(E4M3),
                lhsT_scale=wb_dealt_s[:, t, :], rhs=hid_codes[:].bitcast(E5M2), rhs_scale=hid_scales[:],
                start=True, stop=True,
            )
        for h in range(2):
            nc.vector.scalar_tensor_tensor(
                y[:, 2 * h : 2 * h + 2, :], rs_sb[:, 2 * h : 2 * h + 2, :], 0.5, prod[h][:], ALU.mult, ALU.add
            )
        for h in range(2):
            later = y[:, 2 * h : 2 * h + 2, 1:J]
            nc.vector.scalar_tensor_tensor(later, prod[h][:, :, 0 : J - 1], -0.7, later, ALU.mult, ALU.add)
        nc.sync.dma_start(out=out_0.rearrange("(p t) j -> p t j", t=PACK), in_=y[:])

        y16 = sb("y16", [P, J, PACK], BF16)
        nc.vector.tensor_copy(out=y16[:], in_=y[:].rearrange("p t j -> p j t"))
        y_codes = sb("y_codes", [P, J], U32)
        y_scales = sb("y_scales", [P, J], U8)
        nc.vector.quantize_mx(out=y_codes[:].bitcast(E4M3), scales=y_scales[:], in_=y16[:].rearrange("p j t -> p (j t)"))
        nc.sync.dma_start(out=out_1[0].rearrange("p j t -> p (j t)").bitcast(I32), in_=y_codes[:].bitcast(I32))
        for quad in range(P // QUADRANT):
            queue = nc.scalar if quad % 2 == 0 else nc.sync
            queue.dma_start(
                out=out_2[0, SCALE_ROWS * quad : SCALE_ROWS * (quad + 1), :].bitcast(I32),
                in_=y_scales[QUADRANT * quad : QUADRANT * quad + SCALE_ROWS, :].bitcast(I32),
            )
